import numpy as np
import ml_dtypes


def mxq(x, axis, fmt="e4m3"):
    dtype, down = {"e4m3": (ml_dtypes.float8_e4m3fn, 7), "e5m2": (ml_dtypes.float8_e5m2, 14)}[fmt]
    v = np.moveaxis(np.asarray(x, np.float32).astype(ml_dtypes.bfloat16).astype(np.float64), axis, -1)
    blocks = v.reshape(v.shape[:-1] + (-1, 32))
    amax = np.abs(blocks).max(-1, keepdims=True)
    byte = np.maximum(np.where(amax > 0, np.frexp(amax)[1] - 1 + 127, 0) - down, 1)
    scale = np.exp2(byte - 127.0)
    codes = (blocks / scale).astype(np.float32).astype(dtype).astype(np.float64)
    return np.moveaxis((codes * scale).reshape(v.shape), -1, axis)


WIDE = False


def mx_kscale(k):
    if not WIDE:
        return np.ones(k)
    levels = np.array([10, -10, 5, -5, 0])
    if k % 512:
        return np.exp2(np.random.permutation(np.resize(levels, k // 32))).repeat(32)
    a = np.empty((k // 512, 16))
    for p in range(k // 512):
        a[p, :8] = np.random.permutation(np.resize(levels, 8))
        for g in range(8):
            far = levels[np.abs(levels - a[p, g]) >= 10]
            a[p, g + 8] = far[np.random.randint(len(far))]
    return np.exp2(a.ravel()).repeat(32)


def f64(x):
    return np.asarray(x).astype(np.float64)


def striped(idx):
    return np.tile(idx.reshape(-1, 16).T, (8, 1)).astype(np.uint16)


def unstriped(offs):
    return offs[:16].T.reshape(-1).astype(np.int64)


E2M1 = np.array([0.0, 0.5, 1.0, 1.5, 2.0, 3.0, 4.0, 6.0, -0.0, -0.5, -1.0, -1.5, -2.0, -3.0, -4.0, -6.0])


def pack_weight(w, fmt):
    k, n = w.shape
    w = f64(np.asarray(w, np.float32).astype(ml_dtypes.bfloat16)).reshape(k // 32, 32, n)
    amax = np.abs(w).max(1)
    if fmt == "e4m3":
        byte = np.frexp(amax)[1] - 1 + 127 - 7
    else:
        mant, ex = np.frexp(amax / 6.0)
        byte = np.where(mant > 0.5, ex, ex - 1) + 127
    byte = np.clip(np.where(amax > 0, byte, 1), 1, 254)
    scaled = (w * np.exp2(127.0 - byte)[:, None, :]).reshape(k, n).astype(np.float32)
    by_word = np.ascontiguousarray(scaled.reshape(k // 512, 128, 4, n).transpose(0, 1, 3, 2))
    if fmt == "e4m3":
        words = by_word.astype(ml_dtypes.float8_e4m3fn).view(np.uint8)
    else:
        c = by_word.astype(ml_dtypes.float4_e2m1fn).view(np.uint8) & 0xF
        words = (c[..., 0::2] | (c[..., 1::2] << 4)).reshape(k // 512, 128, 2 * n)
    return np.ascontiguousarray(words), np.ascontiguousarray(byte.astype(np.uint8).reshape(k // 512, 16, n))


def unpack_weight(words, scales, fmt):
    g, _, n = scales.shape
    words = np.ascontiguousarray(words).reshape(g, 128, n, -1)
    if fmt == "e4m3":
        vals = words.view(ml_dtypes.float8_e4m3fn).astype(np.float64)
    else:
        nib = np.empty((g, 128, n, 4), np.uint8)
        nib[..., 0::2] = words & 0xF
        nib[..., 1::2] = words >> 4
        vals = E2M1[nib]
    vals = vals * np.repeat(np.exp2(scales.astype(np.float64) - 127.0), 8, axis=1)[..., None]
    return vals.transpose(0, 1, 3, 2).reshape(g * 512, n)


def gelu(v):
    return 0.5 * v * (1.0 + np.tanh(np.sqrt(2.0 / np.pi) * (v + 0.044715 * v**3)))


def striped8(idx):
    return np.concatenate([v.reshape(-1, 16).T for v in idx]).astype(np.uint16)


def unstriped8(offs):
    return np.stack([offs[16 * g:16 * g + 16].T.reshape(-1) for g in range(8)]).astype(np.int64)


def heads(h, wgt, idx8):
    r = np.arange(h.shape[0])
    return wgt[r // 4 % 128] * h[r[:, None], idx8[r % 512 // 64]]


def put_heads(h, wgs, idx8, t2):
    r = np.arange(h.shape[0])
    page = np.zeros((h.shape[0], t2))
    page[r[:, None], idx8[r % 512 // 64]] = wgs[r // 4 % 128] * h
    return page


K, H, N, T, S, P, T2 = 1024, 1024, 512, 4096, 1024, 512, 1024

def setup_inputs():
    n = np.random.standard_normal
    s = mx_kscale(K)[:, None]
    u = mx_kscale(H)[:, None]
    d = {}
    d["tab_words"], d["tab_scales"] = pack_weight(n((K, T)) * s, "e4m3")
    d["offs"] = striped(np.random.permutation(T)[:S])
    gain = np.random.uniform(0.6, 1.6, H)
    tune = np.random.uniform(0.5, 1.2, H)
    d["w1"] = (0.31 * n((K, H)) / K ** 0.5 / s / (gain * tune)).astype(np.float32)
    d["gain"] = gain.astype(np.float32)
    d["offs2"] = striped8(np.stack([np.random.permutation(S)[:P] for _ in range(8)]))
    d["wgt"] = np.repeat(np.random.uniform(0.5, 2.0, (8, P)), 16, axis=0).astype(np.float32)
    d["tune"] = tune.astype(np.float32)
    d["lift"] = (np.random.uniform(0.7, 1.4, H) * u[:, 0]).astype(np.float32)
    d["w4_words"], d["w4_scales"] = pack_weight(1.22 * n((H, N)) / H ** 0.5 / u, "e2m1")
    d["blend"] = np.random.uniform(0.3, 0.9, N).astype(np.float32)
    d["offs3"] = striped8(np.stack([np.random.permutation(T2)[:P] for _ in range(8)]))
    d["wgo"] = np.repeat(np.random.uniform(0.5, 2.0, (8, P)), 16, axis=0).astype(np.float32)
    return d

def reference(tab_words, tab_scales, offs, w1, gain, offs2, wgt, tune, lift,
              w4_words, w4_scales, blend, offs3, wgo):
    v = unpack_weight(tab_words, tab_scales, "e4m3")[:, unstriped(offs)]
    h = f64(gain)[:, None] * (mxq(f64(w1), 0, "e4m3").T @ v)
    x = heads(h, f64(wgt), unstriped8(offs2))
    b = f64(lift)[:, None] * np.sin(f64(tune)[:, None] * x)
    w4 = unpack_weight(w4_words, w4_scales, "e2m1")
    y = w4.T @ mxq(b, 0, "e4m3")
    y2 = y + f64(blend)[:, None] * np.cos(y)
    return put_heads(y2, f64(wgo), unstriped8(offs3), T2)

@@ -1,0 +1,286 @@
+import math
+from contextlib import ExitStack
+
+import concourse.mybir as mybir
+
+K, H, N, T, S, M, T2 = 1024, 1024, 512, 4096, 1024, 512, 1024
+FLOPS = 2 * K * H * S + 2 * H * N * M
+
+F32 = mybir.dt.float32
+BF16 = mybir.dt.bfloat16
+I32 = mybir.dt.int32
+U32 = mybir.dt.uint32
+U16 = mybir.dt.uint16
+U8 = mybir.dt.uint8
+FP8X4 = mybir.dt.float8_e4m3fn_x4
+FP4X4 = mybir.dt.float4_e2m1fn_x4
+ALU = mybir.AluOpType
+ACT = mybir.ActivationFunctionType
+
+P = 128
+PACK = 4
+BANK = 512
+HALF = M // 2
+TWO_PI = 2.0 * math.pi
+ROUNDER = 1.5 * 2.0**23
+
+
+def tile_list_reed_filing_advice_kernel(tc, tab_words, tab_scales, offs, w1, gain, offs2, wgt, tune, lift,
+                                                  w4_words, w4_scales, blend, offs3, wgo, out):
+    nc = tc.nc
+    with ExitStack() as ctx:
+        lists = ctx.enter_context(tc.tile_pool(name="lists", bufs=1))
+        keep = ctx.enter_context(tc.tile_pool(name="keep", bufs=1))
+        psum = ctx.enter_context(tc.psum_pool(name="psum", bufs=8))
+
+        def sb(name, shape, dtype):
+            return keep.tile(shape, dtype, name=name, align_bytes=64)
+
+        list1 = lists.tile([P, S // 16], U16, name="list1")
+        list2 = lists.tile([P, M // 16], U16, name="list2")
+        list3 = lists.tile([P, M // 16], U16, name="list3")
+
+        tab_sc = sb("tab_sc", [P, T], U8)
+        nc.vector.memset(tab_sc[:].bitcast(I32), 0)
+        w4_sc_raw = sb("w4_sc_raw", [P, 2, N], U8)
+        nc.vector.memset(w4_sc_raw[:].rearrange("p a n -> p (a n)").bitcast(I32), 0)
+        pages = [sb("page%d" % i, [P, T2], F32) for i in range(PACK)]
+        for i in range(PACK):
+            nc.vector.memset(pages[i][:], 0.0)
+        warm = sb("warm", [P, 1], F32)
+        nc.scalar.activation(out=warm[:], in_=pages[0][:, 0:1], func=ACT.Sin)
+
+        nc.sync.dma_start(list1[:], offs)
+        tab = [sb("tab%d" % a, [P, T], I32) for a in range(2)]
+        nc.sync.dma_start(out=tab[0][:], in_=tab_words[0].rearrange("p t i -> p (t i)").bitcast(I32))
+        for q in range(4):
+            nc.sync.dma_start(out=tab_sc[32 * q:32 * q + 8, :].bitcast(I32),
+                              in_=tab_scales[:, 4 * q:4 * q + 4, :].bitcast(I32))
+        nc.sync.dma_start(out=tab[1][:], in_=tab_words[1].rearrange("p t i -> p (t i)").bitcast(I32))
+        w1_raw = {}
+
+        def load_w1(a, b):
+            w1_raw[a, b] = sb("w1_raw%d%d" % (a, b), [P, PACK, BANK], F32)
+            nc.sync.dma_start(out=w1_raw[a, b][:],
+                              in_=w1[512 * a:512 * (a + 1), 512 * b:512 * (b + 1)].rearrange("(p j) c -> p j c", j=PACK))
+
+        load_w1(0, 0)
+        load_w1(1, 0)
+        nc.sync.dma_start(list2[:], offs2)
+        wgt_sb = sb("wgt_sb", [P, M], F32)
+        nc.sync.dma_start(out=wgt_sb[:], in_=wgt)
+        w4_raw = sb("w4_raw", [P, 2, 2 * N], U8)
+        nc.sync.dma_start(out=w4_raw[:].bitcast(I32), in_=w4_words.rearrange("a p n -> p a n").bitcast(I32))
+        load_w1(0, 1)
+        load_w1(1, 1)
+        nc.sync.dma_start(list3[:], offs3)
+        wgo_sb = sb("wgo_sb", [P, M], F32)
+        nc.sync.dma_start(out=wgo_sb[:], in_=wgo)
+
+        def load_rows(name, vec, blocks):
+            t = sb(name, [P, blocks, PACK], F32)
+            nc.gpsimd.dma_start(out=t[:], in_=vec.rearrange("(b p i) -> p b i", p=P, i=PACK))
+            return t
+
+        gain_sb = load_rows("gain_sb", gain, 2)
+        tune_sb = load_rows("tune_sb", tune, 2)
+        for q in range(4):
+            nc.gpsimd.dma_start(out=w4_sc_raw[32 * q:32 * q + 4, :, :].bitcast(I32),
+                                in_=w4_scales[:, 4 * q:4 * q + 4, :].rearrange("a r n -> r a n").bitcast(I32))
+        lift_sb = load_rows("lift_sb", lift, 2)
+        blend_sb = load_rows("blend_sb", blend, 1)
+
+        v_sc = sb("v_sc", [P, S], U8)
+        v = [sb("v%d" % a, [P, S], U32) for a in range(2)]
+        nc.vector.tensor_copy(out=v[0][:], in_=tab[0][:].bitcast(U32).indirect(list1[:]))
+        nc.vector.tensor_copy(out=v_sc[:], in_=tab_sc[:].indirect(list1[:]))
+        nc.vector.tensor_copy(out=v[1][:], in_=tab[1][:].bitcast(U32).indirect(list1[:]))
+
+        turns = sb("turns", [P, 2, PACK], F32)
+        nc.vector.scalar_tensor_tensor(out=turns[:], in0=gain_sb[:], scalar=1.0 / TWO_PI, in1=tune_sb[:],
+                                       op0=ALU.mult, op1=ALU.mult)
+
+        w1_bf, w1_q, w1_sc = {}, {}, {}
+
+        def cast_w1(a, b, u, engine):
+            t = sb("w1_bf%d%d%d" % (a, b, u), [P, 2, P, PACK], BF16)
+            w1_bf[a, b, u] = t
+            src = w1_raw[a, b][:].rearrange("p j (m t) -> p m j t", t=PACK)[:, :, :, 2 * u:2 * u + 2]
+            dst = t[:].rearrange("p t m j -> p m j t")
+            if engine == "vector":
+                nc.vector.tensor_copy(out=dst, in_=src)
+            else:
+                nc.scalar.copy(out=dst, in_=src)
+
+        def quant_w1(a, b, u):
+            w1_q[a, b, u] = sb("w1_q%d%d%d" % (a, b, u), [P, 2 * P], U32)
+            w1_sc[a, b, u] = sb("w1_sc%d%d%d" % (a, b, u), [P, 2 * P], U8)
+            nc.vector.quantize_mx(out=w1_q[a, b, u][:].bitcast(FP8X4), scales=w1_sc[a, b, u][:],
+                                  in_=w1_bf[a, b, u][:].rearrange("p t m j -> p (t m j)"))
+
+        h_ps, h = {}, {}
+
+        def mm1(a, b, i, c):
+            if a == 0:
+                h_ps[b, i, c] = psum.tile([P, BANK], F32, name="bank")
+            cols = slice(P * (i % 2), P * (i % 2 + 1))
+            picks = slice(BANK * c, BANK * (c + 1))
+            nc.tensor.matmul_mx(out=h_ps[b, i, c][:], lhsT=w1_q[a, b, i // 2][:, cols].bitcast(FP8X4),
+                                lhsT_scale=w1_sc[a, b, i // 2][:, cols], rhs=v[a][:, picks].bitcast(FP8X4),
+                                rhs_scale=v_sc[4 * a:P, picks], start=(a == 0), stop=(a == 1))
+
+        def evac_h(b, i):
+            h[b, i] = sb("h%d" % i, [P, S], F32)
+            for c in range(2):
+                nc.scalar.activation(out=h[b, i][:, BANK * c:BANK * (c + 1)], in_=h_ps[b, i, c][:], func=ACT.Copy,
+                                     scale=turns[:, b, i:i + 1])
+
+        for a in range(2):
+            cast_w1(a, 0, 0, "vector")
+            cast_w1(a, 0, 1, "scalar")
+            for u in range(2):
+                quant_w1(a, 0, u)
+                for i in (2 * u, 2 * u + 1):
+                    for c in range(2):
+                        mm1(a, 0, i, c)
+        for i in range(PACK):
+            evac_h(0, i)
+
+        w4_q = sb("w4_q", [P, 2, PACK, P, 2], U8)
+        nc.vector.tensor_copy(out=w4_q[:].rearrange("p a t q e -> p a q t e"),
+                              in_=w4_raw[:].rearrange("p a (q t e) -> p a q t e", t=PACK, e=2))
+        w4_sc = sb("w4_sc", [P, 2, PACK, P], U8)
+        nc.vector.tensor_copy(out=w4_sc[:].rearrange("p a t q -> p a q t"),
+                              in_=w4_sc_raw[:].rearrange("p a (q t) -> p a q t", t=PACK))
+
+        def whole_turns(name, u_ap, shape, engine):
+            t = sb(name, shape, U32)
+            if engine == "vector":
+                nc.vector.tensor_scalar(out=t[:].bitcast(I32), in0=u_ap, scalar1=ROUNDER, scalar2=None, op0=ALU.add)
+            else:
+                nc.scalar.activation(out=t[:], in_=u_ap, func=ACT.Copy, bias=ROUNDER)
+            return t
+
+        def rest(out_ap, k_tile, u_ap):
+            nc.vector.scalar_tensor_tensor(out=out_ap, in0=k_tile[:].bitcast(I32), scalar=ROUNDER, in1=u_ap,
+                                           op0=ALU.subtract, op1=ALU.subtract)
+
+        def sine(name, f_ap, width):
+            s = sb(name, [P, width, PACK], F32)
+            nc.scalar.activation(out=s[:], in_=f_ap.rearrange("p i m -> p m i"), func=ACT.Sin, scale=-TWO_PI)
+            return s
+
+        def lifted(dst_ap, s, b, width):
+            nc.vector.tensor_tensor(out=dst_ap, in0=s[:], in1=lift_sb[:, b:b + 1, :].to_broadcast([P, width, PACK]),
+                                    op=ALU.mult)
+
+        b_q, b_sc = {}, {}
+
+        def quant_b(b, half, src):
+            b_q[b, half] = sb("b_q%d%d" % (b, half), [P, HALF], U32)
+            b_sc[b, half] = sb("b_sc%d%d" % (b, half), [P, HALF], U8)
+            nc.vector.quantize_mx(out=b_q[b, half][:].bitcast(FP8X4), scales=b_sc[b, half][:],
+                                  in_=src[:].rearrange("p m i -> p (m i)"))
+
+        u0 = sb("u0", [P, PACK, M], F32)
+        f0 = u0
+        for a in range(2):
+            for u in range(2):
+                cast_w1(a, 1, u, "scalar")
+        for i in range(PACK):
+            nc.vector.tensor_tensor(out=u0[:, i, :], in0=h[0, i][:].indirect(list2[:]), in1=wgt_sb[:], op=ALU.mult)
+        for i in range(PACK):
+            k0 = whole_turns("k0%d" % i, u0[:, i, :], [P, M], "vector")
+            if i < 2:
+                quant_w1(0, 1, i)
+            rest(f0[:, i, :], k0, u0[:, i, :])
+        for u in range(2):
+            quant_w1(1, 1, u)
+        s0 = [sine("s0%d" % half, f0[:, :, HALF * half:HALF * (half + 1)], HALF) for half in range(2)]
+        for i in range(PACK):
+            for c in range(2):
+                mm1(0, 1, i, c)
+                mm1(1, 1, i, c)
+            evac_h(1, i)
+        for half in range(2):
+            bb = sb("bb0%d" % half, [P, HALF, PACK], BF16)
+            lifted(bb[:], s0[half], 0, HALF)
+            quant_b(0, half, bb)
+
+        u1 = [sb("u1%d" % half, [P, PACK, HALF], F32) for half in range(2)]
+        f1 = u1
+        k1 = {}
+        for half in range(2):
+            for i in range(PACK):
+                nc.vector.tensor_tensor(out=u1[half][:, i, :],
+                                        in0=h[1, i][:].indirect(list2[:, 16 * half:16 * (half + 1)]),
+                                        in1=wgt_sb[:, HALF * half:HALF * (half + 1)], op=ALU.mult)
+            k1[half] = whole_turns("k1%d" % half, u1[half][:].rearrange("p i m -> p (i m)"), [P, PACK * HALF], "scalar")
+        s1 = {}
+        for half in range(2):
+            rest(f1[half][:].rearrange("p i m -> p (i m)"), k1[half], u1[half][:].rearrange("p i m -> p (i m)"))
+            s1[half] = sine("s1%d" % half, f1[half][:], HALF)
+
+        y_ps, y2 = {}, {}
+
+        def second(half):
+            bb = sb("bb1%d" % half, [P, HALF, PACK], BF16)
+            lifted(bb[:], s1[half], 1, HALF)
+            quant_b(1, half, bb)
+            for i in range(PACK):
+                y_ps[half, i] = psum.tile([P, BANK], F32, name="bank")
+                for g in range(2):
+                    cols = slice(P * g, P * (g + 1))
+                    for a in range(2):
+                        nc.tensor.matmul_mx(out=y_ps[half, i][:, cols],
+                                            lhsT=w4_q[:, a, i, :, :].rearrange("p q e -> p (q e)").bitcast(FP4X4),
+                                            lhsT_scale=w4_sc[:, a, i, :], rhs=b_q[a, half][:, cols].bitcast(FP8X4),
+                                            rhs_scale=b_sc[a, half][:, cols], start=(a == 0), stop=(a == 1))
+
+        u2, k2 = {}, {}
+
+        def cos_turns(half, i):
+            u2[half, i] = sb("u2%d%d" % (half, i), [P, HALF], F32)
+            nc.scalar.activation(out=u2[half, i][:], in_=y_ps[half, i][:, 0:HALF], func=ACT.Copy,
+                                 scale=1.0 / TWO_PI, bias=0.25)
+            k2[half, i] = whole_turns("k2%d%d" % (half, i), u2[half, i][:], [P, HALF], "scalar")
+
+        c2 = {}
+
+        def cos_value(half, i):
+            f2 = u2[half, i]
+            rest(f2[:], k2[half, i], u2[half, i][:])
+            c2[half, i] = f2
+            nc.scalar.activation(out=c2[half, i][:], in_=f2[:], func=ACT.Sin, scale=-TWO_PI)
+
+        def blend_in(half, i):
+            y2[half, i] = c2[half, i]
+            nc.vector.scalar_tensor_tensor(out=y2[half, i][:], in0=c2[half, i][:], scalar=blend_sb[:, 0, i:i + 1],
+                                           in1=y_ps[half, i][:, 0:HALF], op0=ALU.mult, op1=ALU.add)
+
+        def put(half, i):
+            nc.vector.tensor_tensor(out=pages[i][:].indirect(list3[:, 16 * half:16 * (half + 1)]), in0=y2[half, i][:],
+                                    in1=wgo_sb[:, HALF * half:HALF * (half + 1)], op=ALU.mult)
+
+        out_rows = out.rearrange("(p i) t -> p i t", i=PACK)
+        second(0)
+        for i in range(PACK):
+            cos_turns(0, i)
+        second(1)
+        for i in range(PACK):
+            cos_value(0, i)
+        for i in range(PACK):
+            cos_turns(1, i)
+        for i in range(PACK):
+            blend_in(0, i)
+        put(0, 0)
+        put(0, 1)
+        for i in range(PACK):
+            cos_value(1, i)
+        put(0, 2)
+        put(0, 3)
+        for i in range(PACK):
+            blend_in(1, i)
+        for i in range(PACK):
+            put(1, i)
+            nc.sync.dma_start(out=out_rows[:, i, :], in_=pages[i][:])

@@ -43,52 +43,55 @@ def tile_list_reed_filing_advice_kernel(tc, tab_words, tab_scales, offs, w1, gai
         tab_sc = sb("tab_sc", [P, T], U8)
         nc.vector.memset(tab_sc[:].bitcast(I32), 0)
         w4_sc_raw = sb("w4_sc_raw", [P, 2, N], U8)
-        nc.vector.memset(w4_sc_raw[:].rearrange("p a n -> p (a n)").bitcast(I32), 0)
+        nc.gpsimd.memset(w4_sc_raw[:].rearrange("p a n -> p (a n)").bitcast(I32), 0)
         pages = [sb("page%d" % i, [P, T2], F32) for i in range(PACK)]
         for i in range(PACK):
             nc.vector.memset(pages[i][:], 0.0)
         warm = sb("warm", [P, 1], F32)
         nc.scalar.activation(out=warm[:], in_=pages[0][:, 0:1], func=ACT.Sin)
 
+        def load_rows(name, vec, blocks):
+            t = sb(name, [P, blocks, PACK], F32)
+            nc.sync.dma_start(out=t[:], in_=vec.rearrange("(b p i) -> p b i", p=P, i=PACK))
+            return t
+
+        w1_raw = {}
+
+        def load_w1(a, b, c0, c1):
+            w1_raw[a, b, c0] = sb("w1_raw%d%d_%d" % (a, b, c0), [P, PACK, c1 - c0], F32)
+            nc.sync.dma_start(out=w1_raw[a, b, c0][:],
+                              in_=w1[512 * a:512 * (a + 1), 512 * b + c0:512 * b + c1].rearrange("(p j) c -> p j c", j=PACK))
+
         nc.sync.dma_start(list1[:], offs)
+        w4_raw = sb("w4_raw", [P, 2, 2 * N], U8)
+        nc.sync.dma_start(out=w4_raw[:].bitcast(I32), in_=w4_words.rearrange("a p n -> p a n").bitcast(I32))
         tab = [sb("tab%d" % a, [P, T], I32) for a in range(2)]
         nc.sync.dma_start(out=tab[0][:], in_=tab_words[0].rearrange("p t i -> p (t i)").bitcast(I32))
         for q in range(4):
             nc.sync.dma_start(out=tab_sc[32 * q:32 * q + 8, :].bitcast(I32),
                               in_=tab_scales[:, 4 * q:4 * q + 4, :].bitcast(I32))
         nc.sync.dma_start(out=tab[1][:], in_=tab_words[1].rearrange("p t i -> p (t i)").bitcast(I32))
-        w1_raw = {}
-
-        def load_w1(a, b):
-            w1_raw[a, b] = sb("w1_raw%d%d" % (a, b), [P, PACK, BANK], F32)
-            nc.sync.dma_start(out=w1_raw[a, b][:],
-                              in_=w1[512 * a:512 * (a + 1), 512 * b:512 * (b + 1)].rearrange("(p j) c -> p j c", j=PACK))
-
-        load_w1(0, 0)
-        load_w1(1, 0)
-        nc.sync.dma_start(list2[:], offs2)
-        wgt_sb = sb("wgt_sb", [P, M], F32)
-        nc.sync.dma_start(out=wgt_sb[:], in_=wgt)
-        w4_raw = sb("w4_raw", [P, 2, 2 * N], U8)
-        nc.sync.dma_start(out=w4_raw[:].bitcast(I32), in_=w4_words.rearrange("a p n -> p a n").bitcast(I32))
-        load_w1(0, 1)
-        load_w1(1, 1)
-        nc.sync.dma_start(list3[:], offs3)
-        wgo_sb = sb("wgo_sb", [P, M], F32)
-        nc.sync.dma_start(out=wgo_sb[:], in_=wgo)
-
-        def load_rows(name, vec, blocks):
-            t = sb(name, [P, blocks, PACK], F32)
-            nc.gpsimd.dma_start(out=t[:], in_=vec.rearrange("(b p i) -> p b i", p=P, i=PACK))
-            return t
-
+        load_w1(0, 0, 0, 512)
+        load_w1(1, 0, 0, 512)
         gain_sb = load_rows("gain_sb", gain, 2)
         tune_sb = load_rows("tune_sb", tune, 2)
         for q in range(4):
             nc.gpsimd.dma_start(out=w4_sc_raw[32 * q:32 * q + 4, :, :].bitcast(I32),
                                 in_=w4_scales[:, 4 * q:4 * q + 4, :].rearrange("a r n -> r a n").bitcast(I32))
+        nc.sync.dma_start(list2[:], offs2)
+        wgt_sb = sb("wgt_sb", [P, M], F32)
+        nc.sync.dma_start(out=wgt_sb[:], in_=wgt)
+        load_w1(0, 1, 0, 512)
+        load_w1(1, 1, 0, 512)
         lift_sb = load_rows("lift_sb", lift, 2)
         blend_sb = load_rows("blend_sb", blend, 1)
+        nc.sync.dma_start(list3[:], offs3)
+        wgo_sb = sb("wgo_sb", [P, M], F32)
+        nc.sync.dma_start(out=wgo_sb[:], in_=wgo)
+
+        w4_q = sb("w4_q", [P, 2, PACK, 2 * P], U8)
+        nc.vector.tensor_copy(out=w4_q[:].bitcast(U16),
+                              in_=w4_raw[:].bitcast(U16).rearrange("p a (q t) -> p a t q", t=PACK))
 
         v_sc = sb("v_sc", [P, S], U8)
         v = [sb("v%d" % a, [P, S], U32) for a in range(2)]
@@ -96,24 +99,27 @@ def tile_list_reed_filing_advice_kernel(tc, tab_words, tab_scales, offs, w1, gai
         nc.vector.tensor_copy(out=v_sc[:], in_=tab_sc[:].indirect(list1[:]))
         nc.vector.tensor_copy(out=v[1][:], in_=tab[1][:].bitcast(U32).indirect(list1[:]))
 
+        w4_sc = sb("tab1", [P, 2, PACK, P], U8)
+        nc.vector.tensor_copy(out=w4_sc[:], in_=w4_sc_raw[:].rearrange("p a (q t) -> p a t q", t=PACK))
+
         turns = sb("turns", [P, 2, PACK], F32)
         nc.vector.scalar_tensor_tensor(out=turns[:], in0=gain_sb[:], scalar=1.0 / TWO_PI, in1=tune_sb[:],
                                        op0=ALU.mult, op1=ALU.mult)
 
         w1_bf, w1_q, w1_sc = {}, {}, {}
 
-        def cast_w1(a, b, u, engine):
-            t = sb("w1_bf%d%d%d" % (a, b, u), [P, 2, P, PACK], BF16)
-            w1_bf[a, b, u] = t
-            src = w1_raw[a, b][:].rearrange("p j (m t) -> p m j t", t=PACK)[:, :, :, 2 * u:2 * u + 2]
-            dst = t[:].rearrange("p t m j -> p m j t")
+        def cast_w1(a, b, u, engine, c0=0, c1=512):
+            if c0 == 0:
+                w1_bf[a, b, u] = sb("w1_bf%d%d%d" % (a, b, u), [P, 2, P, PACK], BF16)
+            src = w1_raw[a, b, c0][:].rearrange("p j (m t) -> p m j t", t=PACK)[:, :, :, 2 * u:2 * u + 2]
+            dst = w1_bf[a, b, u][:, :, c0 // PACK:c1 // PACK, :].rearrange("p t m j -> p m j t")
             if engine == "vector":
                 nc.vector.tensor_copy(out=dst, in_=src)
             else:
                 nc.scalar.copy(out=dst, in_=src)
 
-        def quant_w1(a, b, u):
-            w1_q[a, b, u] = sb("w1_q%d%d%d" % (a, b, u), [P, 2 * P], U32)
+        def quant_w1(a, b, u, name=None):
+            w1_q[a, b, u] = sb(name or "w1_q%d%d%d" % (a, b, u), [P, 2 * P], U32)
             w1_sc[a, b, u] = sb("w1_sc%d%d%d" % (a, b, u), [P, 2 * P], U8)
             nc.vector.quantize_mx(out=w1_q[a, b, u][:].bitcast(FP8X4), scales=w1_sc[a, b, u][:],
                                   in_=w1_bf[a, b, u][:].rearrange("p t m j -> p (t m j)"))
@@ -132,27 +138,35 @@ def tile_list_reed_filing_advice_kernel(tc, tab_words, tab_scales, offs, w1, gai
         def evac_h(b, i):
             h[b, i] = sb("h%d" % i, [P, S], F32)
             for c in range(2):
-                nc.scalar.activation(out=h[b, i][:, BANK * c:BANK * (c + 1)], in_=h_ps[b, i, c][:], func=ACT.Copy,
-                                     scale=turns[:, b, i:i + 1])
+                dst = h[b, i][:, BANK * c:BANK * (c + 1)]
+                if (b, i, c) == (0, 0, 1):
+                    nc.vector.tensor_scalar(out=dst, in0=h_ps[b, i, c][:], scalar1=turns[:, b, i:i + 1], scalar2=None,
+                                            op0=ALU.mult)
+                else:
+                    nc.scalar.activation(out=dst, in_=h_ps[b, i, c][:], func=ACT.Copy, scale=turns[:, b, i:i + 1])
 
-        for a in range(2):
-            cast_w1(a, 0, 0, "vector")
-            cast_w1(a, 0, 1, "scalar")
-            for u in range(2):
-                quant_w1(a, 0, u)
-                for i in (2 * u, 2 * u + 1):
-                    for c in range(2):
-                        mm1(a, 0, i, c)
-        for i in range(PACK):
+        cast_w1(0, 0, 0, "vector")
+        cast_w1(0, 0, 1, "scalar")
+        quant_w1(0, 0, 0)
+        for i in range(2):
+            for c in range(2):
+                mm1(0, 0, i, c)
+        cast_w1(1, 0, 0, "vector")
+        cast_w1(1, 0, 1, "scalar")
+        quant_w1(1, 0, 0)
+        for i in range(2):
+            for c in range(2):
+                mm1(1, 0, i, c)
+        quant_w1(0, 0, 1, "w1_bf100")
+        quant_w1(1, 0, 1)
+        for i in range(2, PACK):
+            for c in range(2):
+                mm1(0, 0, i, c)
+                mm1(1, 0, i, c)
+        for i in range(PACK - 1):
             evac_h(0, i)
-
-        w4_q = sb("w4_q", [P, 2, PACK, P, 2], U8)
-        nc.vector.tensor_copy(out=w4_q[:].rearrange("p a t q e -> p a q t e"),
-                              in_=w4_raw[:].rearrange("p a (q t e) -> p a q t e", t=PACK, e=2))
-        w4_sc = sb("w4_sc", [P, 2, PACK, P], U8)
-        nc.vector.tensor_copy(out=w4_sc[:].rearrange("p a t q -> p a q t"),
-                              in_=w4_sc_raw[:].rearrange("p a (q t) -> p a q t", t=PACK))
-
+        cast_w1(0, 1, 0, "scalar")
+        evac_h(0, PACK - 1)
         def whole_turns(name, u_ap, shape, engine):
             t = sb(name, shape, U32)
             if engine == "vector":
@@ -161,18 +175,20 @@ def tile_list_reed_filing_advice_kernel(tc, tab_words, tab_scales, offs, w1, gai
                 nc.scalar.activation(out=t[:], in_=u_ap, func=ACT.Copy, bias=ROUNDER)
             return t
 
-        def rest(out_ap, k_tile, u_ap):
-            nc.vector.scalar_tensor_tensor(out=out_ap, in0=k_tile[:].bitcast(I32), scalar=ROUNDER, in1=u_ap,
+        def rest(k_ap, u_ap, out_ap=None):
+            nc.vector.scalar_tensor_tensor(out=u_ap if out_ap is None else out_ap, in0=k_ap.bitcast(I32), scalar=ROUNDER, in1=u_ap,
                                            op0=ALU.subtract, op1=ALU.subtract)
 
-        def sine(name, f_ap, width):
-            s = sb(name, [P, width, PACK], F32)
+        def sine_woven(name, f_ap):
+            s = sb(name, [P, HALF, PACK], F32)
             nc.scalar.activation(out=s[:], in_=f_ap.rearrange("p i m -> p m i"), func=ACT.Sin, scale=-TWO_PI)
             return s
 
-        def lifted(dst_ap, s, b, width):
-            nc.vector.tensor_tensor(out=dst_ap, in0=s[:], in1=lift_sb[:, b:b + 1, :].to_broadcast([P, width, PACK]),
+        def lifted(name, s, b):
+            bb = sb(name, [P, HALF, PACK], BF16)
+            nc.vector.tensor_tensor(out=bb[:], in0=s[:], in1=lift_sb[:, b:b + 1, :].to_broadcast([P, HALF, PACK]),
                                     op=ALU.mult)
+            return bb
 
         b_q, b_sc = {}, {}
 
@@ -183,102 +199,105 @@ def tile_list_reed_filing_advice_kernel(tc, tab_words, tab_scales, offs, w1, gai
                                   in_=src[:].rearrange("p m i -> p (m i)"))
 
         u0 = sb("u0", [P, PACK, M], F32)
-        f0 = u0
-        for a in range(2):
-            for u in range(2):
-                cast_w1(a, 1, u, "scalar")
+        cast_w1(0, 1, 1, "scalar")
+        cast_w1(1, 1, 1, "scalar")
         for i in range(PACK):
             nc.vector.tensor_tensor(out=u0[:, i, :], in0=h[0, i][:].indirect(list2[:]), in1=wgt_sb[:], op=ALU.mult)
-        for i in range(PACK):
-            k0 = whole_turns("k0%d" % i, u0[:, i, :], [P, M], "vector")
-            if i < 2:
-                quant_w1(0, 1, i)
-            rest(f0[:, i, :], k0, u0[:, i, :])
+        cast_w1(1, 1, 0, "vector")
         for u in range(2):
-            quant_w1(1, 1, u)
-        s0 = [sine("s0%d" % half, f0[:, :, HALF * half:HALF * (half + 1)], HALF) for half in range(2)]
+            for a in range(2):
+                quant_w1(a, 1, u)
         for i in range(PACK):
             for c in range(2):
                 mm1(0, 1, i, c)
                 mm1(1, 1, i, c)
             evac_h(1, i)
-        for half in range(2):
-            bb = sb("bb0%d" % half, [P, HALF, PACK], BF16)
-            lifted(bb[:], s0[half], 0, HALF)
-            quant_b(0, half, bb)
+        k00 = whole_turns("w1_bf110", u0[:, :, 0:HALF], [P, PACK, HALF], "vector")
+        rest(k00[:], u0[:, :, 0:HALF])
+        k01 = whole_turns("k01", u0[:, :, HALF:M], [P, PACK, HALF], "scalar")
+        s0 = sine_woven("s0", u0[:, :, 0:HALF])
 
-        u1 = [sb("u1%d" % half, [P, PACK, HALF], F32) for half in range(2)]
-        f1 = u1
-        k1 = {}
-        for half in range(2):
-            for i in range(PACK):
-                nc.vector.tensor_tensor(out=u1[half][:, i, :],
-                                        in0=h[1, i][:].indirect(list2[:, 16 * half:16 * (half + 1)]),
-                                        in1=wgt_sb[:, HALF * half:HALF * (half + 1)], op=ALU.mult)
-            k1[half] = whole_turns("k1%d" % half, u1[half][:].rearrange("p i m -> p (i m)"), [P, PACK * HALF], "scalar")
-        s1 = {}
-        for half in range(2):
-            rest(f1[half][:].rearrange("p i m -> p (i m)"), k1[half], u1[half][:].rearrange("p i m -> p (i m)"))
-            s1[half] = sine("s1%d" % half, f1[half][:], HALF)
+        y_ps = {}
 
-        y_ps, y2 = {}, {}
-
-        def second(half):
-            bb = sb("bb1%d" % half, [P, HALF, PACK], BF16)
-            lifted(bb[:], s1[half], 1, HALF)
-            quant_b(1, half, bb)
-            for i in range(PACK):
-                y_ps[half, i] = psum.tile([P, BANK], F32, name="bank")
-                for g in range(2):
-                    cols = slice(P * g, P * (g + 1))
-                    for a in range(2):
-                        nc.tensor.matmul_mx(out=y_ps[half, i][:, cols],
-                                            lhsT=w4_q[:, a, i, :, :].rearrange("p q e -> p (q e)").bitcast(FP4X4),
+        def second(half, a):
+            for pair in range(2):
+                if a == 0:
+                    y_ps[half, pair] = psum.tile([P, 2, HALF], F32, name="bank")
+                for i in (2 * pair, 2 * pair + 1):
+                    for g in range(2):
+                        cols = slice(P * g, P * (g + 1))
+                        nc.tensor.matmul_mx(out=y_ps[half, pair][:, i % 2, cols], lhsT=w4_q[:, a, i, :].bitcast(FP4X4),
                                             lhsT_scale=w4_sc[:, a, i, :], rhs=b_q[a, half][:, cols].bitcast(FP8X4),
-                                            rhs_scale=b_sc[a, half][:, cols], start=(a == 0), stop=(a == 1))
+                                            rhs_scale=b_sc[a, half][:, cols],
+                                            start=(a == 0 and i % 2 == 0 and g == 0),
+                                            stop=(a == 1 and i % 2 == 1 and g == 1))
 
         u2, k2 = {}, {}
 
-        def cos_turns(half, i):
-            u2[half, i] = sb("u2%d%d" % (half, i), [P, HALF], F32)
-            nc.scalar.activation(out=u2[half, i][:], in_=y_ps[half, i][:, 0:HALF], func=ACT.Copy,
+        def cos_turns(half, pair, engine):
+            u2[half, pair] = sb("u2%d%d" % (half, pair), [P, 2, HALF], F32)
+            nc.scalar.activation(out=u2[half, pair][:], in_=y_ps[half, pair][:], func=ACT.Copy,
                                  scale=1.0 / TWO_PI, bias=0.25)
-            k2[half, i] = whole_turns("k2%d%d" % (half, i), u2[half, i][:], [P, HALF], "scalar")
+            k2[half, pair] = whole_turns("k2%d%d" % (half, pair), u2[half, pair][:], [P, 2, HALF], engine)
 
-        c2 = {}
+        def cos_value(half, pair):
+            rest(k2[half, pair][:], u2[half, pair][:])
+            nc.scalar.activation(out=u2[half, pair][:], in_=u2[half, pair][:], func=ACT.Sin, scale=-TWO_PI)
 
-        def cos_value(half, i):
-            f2 = u2[half, i]
-            rest(f2[:], k2[half, i], u2[half, i][:])
-            c2[half, i] = f2
-            nc.scalar.activation(out=c2[half, i][:], in_=f2[:], func=ACT.Sin, scale=-TWO_PI)
+        y2 = {}
 
-        def blend_in(half, i):
-            y2[half, i] = c2[half, i]
-            nc.vector.scalar_tensor_tensor(out=y2[half, i][:], in0=c2[half, i][:], scalar=blend_sb[:, 0, i:i + 1],
-                                           in1=y_ps[half, i][:, 0:HALF], op0=ALU.mult, op1=ALU.add)
+        def blend_in(half, i, name=None):
+            c = u2[half, i // 2][:, i % 2, :]
+            y2[half, i] = c if name is None else sb(name, [P, HALF], F32)[:]
+            nc.vector.scalar_tensor_tensor(out=y2[half, i], in0=c, scalar=blend_sb[:, 0, i:i + 1],
+                                           in1=y_ps[half, i // 2][:, i % 2, :], op0=ALU.mult, op1=ALU.add)
 
         def put(half, i):
-            nc.vector.tensor_tensor(out=pages[i][:].indirect(list3[:, 16 * half:16 * (half + 1)]), in0=y2[half, i][:],
+            nc.vector.tensor_tensor(out=pages[i][:].indirect(list3[:, 16 * half:16 * (half + 1)]), in0=y2[half, i],
                                     in1=wgo_sb[:, HALF * half:HALF * (half + 1)], op=ALU.mult)
 
         out_rows = out.rearrange("(p i) t -> p i t", i=PACK)
-        second(0)
+        u1 = sb("u1", [P, PACK, M], F32)
         for i in range(PACK):
-            cos_turns(0, i)
-        second(1)
+            nc.vector.tensor_tensor(out=u1[:, i, :], in0=h[1, i][:].indirect(list2[:]), in1=wgt_sb[:], op=ALU.mult)
+        k10 = whole_turns("k10", u1[:, :, 0:HALF], [P, PACK, HALF], "scalar")
+        f01 = sb("h3", [P, PACK, HALF], F32)
+        rest(k01[:], u0[:, :, HALF:M], f01[:])
+        rest(k10[:], u1[:, :, 0:HALF])
+        quant_b(0, 0, lifted("bb00", s0, 0))
+        second(0, 0)
+        k11 = whole_turns("k11", u1[:, :, HALF:M], [P, PACK, HALF], "scalar")
+        s10 = sine_woven("s10", u1[:, :, 0:HALF])
+        nc.scalar.activation(out=f01[:], in_=f01[:], func=ACT.Sin, scale=-TWO_PI)
+        rest(k11[:], u1[:, :, HALF:M])
+        quant_b(1, 0, lifted("bb10", s10, 1))
+        second(0, 1)
+        s11 = sine_woven("s11", u1[:, :, HALF:M])
+        planes = sb("planes", [P, PACK, HALF], BF16)
         for i in range(PACK):
-            cos_value(0, i)
-        for i in range(PACK):
-            cos_turns(1, i)
-        for i in range(PACK):
-            blend_in(0, i)
+            nc.scalar.activation(out=planes[:, i, :], in_=f01[:, i, :], func=ACT.Copy, scale=lift_sb[:, 0, i:i + 1])
+        for pair in range(2):
+            cos_turns(0, pair, "vector")
+        quant_b(1, 1, lifted("bb10", s11, 1))
+        for pair in range(2):
+            cos_value(0, pair)
+        bb01 = sb("bb10", [P, HALF, PACK], BF16)
+        nc.scalar.copy(out=bb01[:], in_=planes[:].rearrange("p i m -> p m i"))
+        blend_in(0, 0)
+        blend_in(0, 1)
         put(0, 0)
+        quant_b(0, 1, bb01)
+        second(1, 0)
+        second(1, 1)
+        for pair in range(2):
+            cos_turns(1, pair, "scalar")
         put(0, 1)
-        for i in range(PACK):
-            cos_value(1, i)
-        put(0, 2)
+        blend_in(0, 3)
+        for pair in range(2):
+            cos_value(1, pair)
         put(0, 3)
+        blend_in(0, 2, "k211")
+        put(0, 2)
         for i in range(PACK):
             blend_in(1, i)
         for i in range(PACK):

import math
from contextlib import ExitStack

import concourse.mybir as mybir

K, H, N, T, S, M, T2 = 1024, 1024, 512, 4096, 1024, 512, 1024
FLOPS = 2 * K * H * S + 2 * H * N * M

F32 = mybir.dt.float32
BF16 = mybir.dt.bfloat16
I32 = mybir.dt.int32
U32 = mybir.dt.uint32
U16 = mybir.dt.uint16
U8 = mybir.dt.uint8
FP8X4 = mybir.dt.float8_e4m3fn_x4
FP4X4 = mybir.dt.float4_e2m1fn_x4
ALU = mybir.AluOpType
ACT = mybir.ActivationFunctionType

P = 128
PACK = 4
BANK = 512
HALF = M // 2
TWO_PI = 2.0 * math.pi
ROUNDER = 1.5 * 2.0**23


def tile_list_reed_filing_advice_kernel(tc, tab_words, tab_scales, offs, w1, gain, offs2, wgt, tune, lift,
                                                  w4_words, w4_scales, blend, offs3, wgo, out):
    nc = tc.nc
    with ExitStack() as ctx:
        lists = ctx.enter_context(tc.tile_pool(name="lists", bufs=1))
        keep = ctx.enter_context(tc.tile_pool(name="keep", bufs=1))
        psum = ctx.enter_context(tc.psum_pool(name="psum", bufs=8))

        def sb(name, shape, dtype):
            return keep.tile(shape, dtype, name=name, align_bytes=64)

        list1 = lists.tile([P, S // 16], U16, name="list1")
        list2 = lists.tile([P, M // 16], U16, name="list2")
        list3 = lists.tile([P, M // 16], U16, name="list3")

        tab_sc = sb("tab_sc", [P, T], U8)
        nc.vector.memset(tab_sc[:].bitcast(I32), 0)
        w4_sc_raw = sb("w4_sc_raw", [P, 2, N], U8)
        nc.gpsimd.memset(w4_sc_raw[:].rearrange("p a n -> p (a n)").bitcast(I32), 0)
        pages = [sb("page%d" % i, [P, T2], F32) for i in range(PACK)]
        for i in range(PACK):
            nc.vector.memset(pages[i][:], 0.0)
        warm = sb("warm", [P, 1], F32)
        nc.scalar.activation(out=warm[:], in_=pages[0][:, 0:1], func=ACT.Sin)

        def load_rows(name, vec, blocks):
            t = sb(name, [P, blocks, PACK], F32)
            nc.sync.dma_start(out=t[:], in_=vec.rearrange("(b p i) -> p b i", p=P, i=PACK))
            return t

        w1_raw = {}

        def load_w1(a, b, c0, c1):
            w1_raw[a, b, c0] = sb("w1_raw%d%d_%d" % (a, b, c0), [P, PACK, c1 - c0], F32)
            nc.sync.dma_start(out=w1_raw[a, b, c0][:],
                              in_=w1[512 * a:512 * (a + 1), 512 * b + c0:512 * b + c1].rearrange("(p j) c -> p j c", j=PACK))

        nc.sync.dma_start(list1[:], offs)
        w4_raw = sb("w4_raw", [P, 2, 2 * N], U8)
        nc.sync.dma_start(out=w4_raw[:].bitcast(I32), in_=w4_words.rearrange("a p n -> p a n").bitcast(I32))
        tab = [sb("tab%d" % a, [P, T], I32) for a in range(2)]
        nc.sync.dma_start(out=tab[0][:], in_=tab_words[0].rearrange("p t i -> p (t i)").bitcast(I32))
        for q in range(4):
            nc.sync.dma_start(out=tab_sc[32 * q:32 * q + 8, :].bitcast(I32),
                              in_=tab_scales[:, 4 * q:4 * q + 4, :].bitcast(I32))
        nc.sync.dma_start(out=tab[1][:], in_=tab_words[1].rearrange("p t i -> p (t i)").bitcast(I32))
        load_w1(0, 0, 0, 512)
        load_w1(1, 0, 0, 512)
        gain_sb = load_rows("gain_sb", gain, 2)
        tune_sb = load_rows("tune_sb", tune, 2)
        for q in range(4):
            nc.gpsimd.dma_start(out=w4_sc_raw[32 * q:32 * q + 4, :, :].bitcast(I32),
                                in_=w4_scales[:, 4 * q:4 * q + 4, :].rearrange("a r n -> r a n").bitcast(I32))
        nc.sync.dma_start(list2[:], offs2)
        wgt_sb = sb("wgt_sb", [P, M], F32)
        nc.sync.dma_start(out=wgt_sb[:], in_=wgt)
        load_w1(0, 1, 0, 512)
        load_w1(1, 1, 0, 512)
        lift_sb = load_rows("lift_sb", lift, 2)
        blend_sb = load_rows("blend_sb", blend, 1)
        nc.sync.dma_start(list3[:], offs3)
        wgo_sb = sb("wgo_sb", [P, M], F32)
        nc.sync.dma_start(out=wgo_sb[:], in_=wgo)

        w4_q = sb("w4_q", [P, 2, PACK, 2 * P], U8)
        nc.vector.tensor_copy(out=w4_q[:].bitcast(U16),
                              in_=w4_raw[:].bitcast(U16).rearrange("p a (q t) -> p a t q", t=PACK))

        v_sc = sb("v_sc", [P, S], U8)
        v = [sb("v%d" % a, [P, S], U32) for a in range(2)]
        nc.vector.tensor_copy(out=v[0][:], in_=tab[0][:].bitcast(U32).indirect(list1[:]))
        nc.vector.tensor_copy(out=v_sc[:], in_=tab_sc[:].indirect(list1[:]))
        nc.vector.tensor_copy(out=v[1][:], in_=tab[1][:].bitcast(U32).indirect(list1[:]))

        w4_sc = sb("tab1", [P, 2, PACK, P], U8)
        nc.vector.tensor_copy(out=w4_sc[:], in_=w4_sc_raw[:].rearrange("p a (q t) -> p a t q", t=PACK))

        turns = sb("turns", [P, 2, PACK], F32)
        nc.vector.scalar_tensor_tensor(out=turns[:], in0=gain_sb[:], scalar=1.0 / TWO_PI, in1=tune_sb[:],
                                       op0=ALU.mult, op1=ALU.mult)

        w1_bf, w1_q, w1_sc = {}, {}, {}

        def cast_w1(a, b, u, engine, c0=0, c1=512):
            if c0 == 0:
                w1_bf[a, b, u] = sb("w1_bf%d%d%d" % (a, b, u), [P, 2, P, PACK], BF16)
            src = w1_raw[a, b, c0][:].rearrange("p j (m t) -> p m j t", t=PACK)[:, :, :, 2 * u:2 * u + 2]
            dst = w1_bf[a, b, u][:, :, c0 // PACK:c1 // PACK, :].rearrange("p t m j -> p m j t")
            if engine == "vector":
                nc.vector.tensor_copy(out=dst, in_=src)
            else:
                nc.scalar.copy(out=dst, in_=src)

        def quant_w1(a, b, u, name=None):
            w1_q[a, b, u] = sb(name or "w1_q%d%d%d" % (a, b, u), [P, 2 * P], U32)
            w1_sc[a, b, u] = sb("w1_sc%d%d%d" % (a, b, u), [P, 2 * P], U8)
            nc.vector.quantize_mx(out=w1_q[a, b, u][:].bitcast(FP8X4), scales=w1_sc[a, b, u][:],
                                  in_=w1_bf[a, b, u][:].rearrange("p t m j -> p (t m j)"))

        h_ps, h = {}, {}

        def mm1(a, b, i, c):
            if a == 0:
                h_ps[b, i, c] = psum.tile([P, BANK], F32, name="bank")
            cols = slice(P * (i % 2), P * (i % 2 + 1))
            picks = slice(BANK * c, BANK * (c + 1))
            nc.tensor.matmul_mx(out=h_ps[b, i, c][:], lhsT=w1_q[a, b, i // 2][:, cols].bitcast(FP8X4),
                                lhsT_scale=w1_sc[a, b, i // 2][:, cols], rhs=v[a][:, picks].bitcast(FP8X4),
                                rhs_scale=v_sc[4 * a:P, picks], start=(a == 0), stop=(a == 1))

        def evac_h(b, i):
            h[b, i] = sb("h%d" % i, [P, S], F32)
            for c in range(2):
                dst = h[b, i][:, BANK * c:BANK * (c + 1)]
                if (b, i, c) == (0, 0, 1):
                    nc.vector.tensor_scalar(out=dst, in0=h_ps[b, i, c][:], scalar1=turns[:, b, i:i + 1], scalar2=None,
                                            op0=ALU.mult)
                else:
                    nc.scalar.activation(out=dst, in_=h_ps[b, i, c][:], func=ACT.Copy, scale=turns[:, b, i:i + 1])

        cast_w1(0, 0, 0, "vector")
        cast_w1(0, 0, 1, "scalar")
        quant_w1(0, 0, 0)
        for i in range(2):
            for c in range(2):
                mm1(0, 0, i, c)
        cast_w1(1, 0, 0, "vector")
        cast_w1(1, 0, 1, "scalar")
        quant_w1(1, 0, 0)
        for i in range(2):
            for c in range(2):
                mm1(1, 0, i, c)
        quant_w1(0, 0, 1, "w1_bf100")
        quant_w1(1, 0, 1)
        for i in range(2, PACK):
            for c in range(2):
                mm1(0, 0, i, c)
                mm1(1, 0, i, c)
        for i in range(PACK - 1):
            evac_h(0, i)
        cast_w1(0, 1, 0, "scalar")
        evac_h(0, PACK - 1)
        def whole_turns(name, u_ap, shape, engine):
            t = sb(name, shape, U32)
            if engine == "vector":
                nc.vector.tensor_scalar(out=t[:].bitcast(I32), in0=u_ap, scalar1=ROUNDER, scalar2=None, op0=ALU.add)
            else:
                nc.scalar.activation(out=t[:], in_=u_ap, func=ACT.Copy, bias=ROUNDER)
            return t

        def rest(k_ap, u_ap, out_ap=None):
            nc.vector.scalar_tensor_tensor(out=u_ap if out_ap is None else out_ap, in0=k_ap.bitcast(I32), scalar=ROUNDER, in1=u_ap,
                                           op0=ALU.subtract, op1=ALU.subtract)

        def sine_woven(name, f_ap):
            s = sb(name, [P, HALF, PACK], F32)
            nc.scalar.activation(out=s[:], in_=f_ap.rearrange("p i m -> p m i"), func=ACT.Sin, scale=-TWO_PI)
            return s

        def lifted(name, s, b):
            bb = sb(name, [P, HALF, PACK], BF16)
            nc.vector.tensor_tensor(out=bb[:], in0=s[:], in1=lift_sb[:, b:b + 1, :].to_broadcast([P, HALF, PACK]),
                                    op=ALU.mult)
            return bb

        b_q, b_sc = {}, {}

        def quant_b(b, half, src):
            b_q[b, half] = sb("b_q%d%d" % (b, half), [P, HALF], U32)
            b_sc[b, half] = sb("b_sc%d%d" % (b, half), [P, HALF], U8)
            nc.vector.quantize_mx(out=b_q[b, half][:].bitcast(FP8X4), scales=b_sc[b, half][:],
                                  in_=src[:].rearrange("p m i -> p (m i)"))

        u0 = sb("u0", [P, PACK, M], F32)
        cast_w1(0, 1, 1, "scalar")
        cast_w1(1, 1, 1, "scalar")
        for i in range(PACK):
            nc.vector.tensor_tensor(out=u0[:, i, :], in0=h[0, i][:].indirect(list2[:]), in1=wgt_sb[:], op=ALU.mult)
        cast_w1(1, 1, 0, "vector")
        for u in range(2):
            for a in range(2):
                quant_w1(a, 1, u)
        for i in range(PACK):
            for c in range(2):
                mm1(0, 1, i, c)
                mm1(1, 1, i, c)
            evac_h(1, i)
        k00 = whole_turns("w1_bf110", u0[:, :, 0:HALF], [P, PACK, HALF], "vector")
        rest(k00[:], u0[:, :, 0:HALF])
        k01 = whole_turns("k01", u0[:, :, HALF:M], [P, PACK, HALF], "scalar")
        s0 = sine_woven("s0", u0[:, :, 0:HALF])

        y_ps = {}

        def second(half, a):
            for pair in range(2):
                if a == 0:
                    y_ps[half, pair] = psum.tile([P, 2, HALF], F32, name="bank")
                for i in (2 * pair, 2 * pair + 1):
                    for g in range(2):
                        cols = slice(P * g, P * (g + 1))
                        nc.tensor.matmul_mx(out=y_ps[half, pair][:, i % 2, cols], lhsT=w4_q[:, a, i, :].bitcast(FP4X4),
                                            lhsT_scale=w4_sc[:, a, i, :], rhs=b_q[a, half][:, cols].bitcast(FP8X4),
                                            rhs_scale=b_sc[a, half][:, cols],
                                            start=(a == 0 and i % 2 == 0 and g == 0),
                                            stop=(a == 1 and i % 2 == 1 and g == 1))

        u2, k2 = {}, {}

        def cos_turns(half, pair, engine):
            u2[half, pair] = sb("u2%d%d" % (half, pair), [P, 2, HALF], F32)
            nc.scalar.activation(out=u2[half, pair][:], in_=y_ps[half, pair][:], func=ACT.Copy,
                                 scale=1.0 / TWO_PI, bias=0.25)
            k2[half, pair] = whole_turns("k2%d%d" % (half, pair), u2[half, pair][:], [P, 2, HALF], engine)

        def cos_value(half, pair):
            rest(k2[half, pair][:], u2[half, pair][:])
            nc.scalar.activation(out=u2[half, pair][:], in_=u2[half, pair][:], func=ACT.Sin, scale=-TWO_PI)

        y2 = {}

        def blend_in(half, i, name=None):
            c = u2[half, i // 2][:, i % 2, :]
            y2[half, i] = c if name is None else sb(name, [P, HALF], F32)[:]
            nc.vector.scalar_tensor_tensor(out=y2[half, i], in0=c, scalar=blend_sb[:, 0, i:i + 1],
                                           in1=y_ps[half, i // 2][:, i % 2, :], op0=ALU.mult, op1=ALU.add)

        def put(half, i):
            nc.vector.tensor_tensor(out=pages[i][:].indirect(list3[:, 16 * half:16 * (half + 1)]), in0=y2[half, i],
                                    in1=wgo_sb[:, HALF * half:HALF * (half + 1)], op=ALU.mult)

        out_rows = out.rearrange("(p i) t -> p i t", i=PACK)
        u1 = sb("u1", [P, PACK, M], F32)
        for i in range(PACK):
            nc.vector.tensor_tensor(out=u1[:, i, :], in0=h[1, i][:].indirect(list2[:]), in1=wgt_sb[:], op=ALU.mult)
        k10 = whole_turns("k10", u1[:, :, 0:HALF], [P, PACK, HALF], "scalar")
        f01 = sb("h3", [P, PACK, HALF], F32)
        rest(k01[:], u0[:, :, HALF:M], f01[:])
        rest(k10[:], u1[:, :, 0:HALF])
        quant_b(0, 0, lifted("bb00", s0, 0))
        second(0, 0)
        k11 = whole_turns("k11", u1[:, :, HALF:M], [P, PACK, HALF], "scalar")
        s10 = sine_woven("s10", u1[:, :, 0:HALF])
        nc.scalar.activation(out=f01[:], in_=f01[:], func=ACT.Sin, scale=-TWO_PI)
        rest(k11[:], u1[:, :, HALF:M])
        quant_b(1, 0, lifted("bb10", s10, 1))
        second(0, 1)
        s11 = sine_woven("s11", u1[:, :, HALF:M])
        planes = sb("planes", [P, PACK, HALF], BF16)
        for i in range(PACK):
            nc.scalar.activation(out=planes[:, i, :], in_=f01[:, i, :], func=ACT.Copy, scale=lift_sb[:, 0, i:i + 1])
        for pair in range(2):
            cos_turns(0, pair, "vector")
        quant_b(1, 1, lifted("bb10", s11, 1))
        for pair in range(2):
            cos_value(0, pair)
        bb01 = sb("bb10", [P, HALF, PACK], BF16)
        nc.scalar.copy(out=bb01[:], in_=planes[:].rearrange("p i m -> p m i"))
        blend_in(0, 0)
        blend_in(0, 1)
        put(0, 0)
        quant_b(0, 1, bb01)
        second(1, 0)
        second(1, 1)
        for pair in range(2):
            cos_turns(1, pair, "scalar")
        put(0, 1)
        blend_in(0, 3)
        for pair in range(2):
            cos_value(1, pair)
        put(0, 3)
        blend_in(0, 2, "k211")
        put(0, 2)
        for i in range(PACK):
            blend_in(1, i)
        for i in range(PACK):
            put(1, i)
            nc.sync.dma_start(out=out_rows[:, i, :], in_=pages[i][:])
